import numpy as np
import ml_dtypes


def mxq(x, axis, fmt="e4m3"):
    dtype, down = {"e4m3": (ml_dtypes.float8_e4m3fn, 7), "e5m2": (ml_dtypes.float8_e5m2, 14)}[fmt]
    v = np.moveaxis(np.asarray(x, np.float32).astype(ml_dtypes.bfloat16).astype(np.float64), axis, -1)
    blocks = v.reshape(v.shape[:-1] + (-1, 32))
    amax = np.abs(blocks).max(-1, keepdims=True)
    byte = np.maximum(np.where(amax > 0, np.frexp(amax)[1] - 1 + 127, 0) - down, 1)
    scale = np.exp2(byte - 127.0)
    codes = (blocks / scale).astype(np.float32).astype(dtype).astype(np.float64)
    return np.moveaxis((codes * scale).reshape(v.shape), -1, axis)


WIDE = False


def mx_kscale(k):
    if not WIDE:
        return np.ones(k)
    levels = np.array([10, -10, 5, -5, 0])
    if k % 512:
        return np.exp2(np.random.permutation(np.resize(levels, k // 32))).repeat(32)
    a = np.empty((k // 512, 16))
    for p in range(k // 512):
        a[p, :8] = np.random.permutation(np.resize(levels, 8))
        for g in range(8):
            far = levels[np.abs(levels - a[p, g]) >= 10]
            a[p, g + 8] = far[np.random.randint(len(far))]
    return np.exp2(a.ravel()).repeat(32)


def f64(x):
    return np.asarray(x).astype(np.float64)


def striped(idx):
    return np.tile(idx.reshape(-1, 16).T, (8, 1)).astype(np.uint16)


def unstriped(offs):
    return offs[:16].T.reshape(-1).astype(np.int64)


def pack_weight(w):
    k, n = w.shape
    w = f64(np.asarray(w, np.float32).astype(ml_dtypes.bfloat16)).reshape(k // 32, 32, n)
    amax = np.abs(w).max(1)
    byte = np.clip(np.where(amax > 0, np.frexp(amax)[1] - 1 + 127 - 7, 1), 1, 254)
    scaled = (w * np.exp2(127.0 - byte)[:, None, :]).reshape(k, n).astype(np.float32)
    words = np.ascontiguousarray(scaled.reshape(k // 512, 128, 4, n).transpose(0, 1, 3, 2)).astype(ml_dtypes.float8_e4m3fn).view(np.uint8)
    return words, np.ascontiguousarray(byte.astype(np.uint8).reshape(k // 512, 16, n))


def unpack_weight(words, scales):
    g, p, n, _ = words.shape
    vals = np.ascontiguousarray(words).view(ml_dtypes.float8_e4m3fn).astype(np.float64) * np.repeat(np.exp2(scales.astype(np.float64) - 127.0), 8, axis=1)[..., None]
    return vals.transpose(0, 1, 3, 2).reshape(g * 512, n)


E2M1 = np.array([0.0, 0.5, 1.0, 1.5, 2.0, 3.0, 4.0, 6.0, -0.0, -0.5, -1.0, -1.5, -2.0, -3.0, -4.0, -6.0])


def pack_fp4(w):
    k, n = w.shape
    w = f64(np.asarray(w, np.float32).astype(ml_dtypes.bfloat16)).reshape(k // 32, 32, n)
    amax = np.abs(w).max(1)
    mant, ex = np.frexp(amax / 6.0)
    byte = np.clip(np.where(amax > 0, np.where(mant > 0.5, ex, ex - 1) + 127, 1), 1, 254)
    scaled = (w * np.exp2(127.0 - byte)[:, None, :]).reshape(k, n).astype(np.float32)
    c = np.ascontiguousarray(scaled.reshape(k // 512, 128, 4, n).transpose(0, 1, 3, 2)).astype(ml_dtypes.float4_e2m1fn).view(np.uint8) & 0xF
    words = (c[..., 0::2] | (c[..., 1::2] << 4)).reshape(k // 512, 128, 2 * n)
    return np.ascontiguousarray(words), np.ascontiguousarray(byte.astype(np.uint8).reshape(k // 512, 16, n))


def unpack_fp4(words, scales):
    g, _, n = scales.shape
    words = np.ascontiguousarray(words).reshape(g, 128, n, 2)
    nib = np.empty((g, 128, n, 4), np.uint8)
    nib[..., 0::2] = words & 0xF
    nib[..., 1::2] = words >> 4
    vals = E2M1[nib] * np.repeat(np.exp2(scales.astype(np.float64) - 127.0), 8, axis=1)[..., None]
    return vals.transpose(0, 1, 3, 2).reshape(g * 512, n)


def relu(v):
    return np.maximum(v, 0.0)

def planes(y):
    n, m = y.shape
    v = y.astype(np.float32).astype(ml_dtypes.bfloat16).astype(np.float64).reshape(n // 32, 32, m)
    top = np.abs(v).max(1)
    byte = np.clip(np.where(top > 0, np.frexp(top)[1] - 1 + 127 - 7, 1), 1, 254)
    codes = (v * np.exp2(127.0 - byte)[:, None, :]).reshape(n, m).astype(np.float32).astype(ml_dtypes.float8_e4m3fn).view(np.uint8)
    words = codes.reshape(n // 512, 128, 4, m).transpose(0, 1, 3, 2)
    return np.ascontiguousarray(words), np.ascontiguousarray(byte.astype(np.uint8).reshape(n // 512, 16, m))


K, T, S, V, H = 512, 1024, 512, 256, 512


def setup_inputs():
    n = np.random.standard_normal
    s = mx_kscale(K)[:, None]
    u = mx_kscale(H)
    packed_xT = pack_weight(n((K, T)) * s)
    packed_w2 = pack_fp4(n((H, H)) / np.sqrt(H) / u[:, None])
    return {
        "x_words": packed_xT[0],
        "x_scales": packed_xT[1],
        "w1": (n((K, H)) / np.sqrt(K) / s * u).astype(np.float32),
        "w2_words": packed_w2[0],
        "w2_scales": packed_w2[1],
        "offs": striped(np.random.permutation(T)[:S]),
    }


def reference(x_words, x_scales, w1, w2_words, w2_scales, offs):
    xq = unpack_weight(x_words, x_scales)[:, unstriped(offs)]
    h = relu(mxq(f64(w1), 0, "e4m3").T @ xq)
    z = np.abs(h[:, :V] - h[:, V:2 * V])
    out_0 = unpack_fp4(w2_words, w2_scales).T @ mxq(z, 0, "e4m3")
    return (out_0,) + planes(out_0)

@@ -1,0 +1,126 @@
+from contextlib import ExitStack
+
+import concourse.mybir as mybir
+
+F32 = mybir.dt.float32
+BF16 = mybir.dt.bfloat16
+I32 = mybir.dt.int32
+U32 = mybir.dt.uint32
+U16 = mybir.dt.uint16
+U8 = mybir.dt.uint8
+FP8X4 = mybir.dt.float8_e4m3fn_x4
+FP4X4 = mybir.dt.float4_e2m1fn_x4
+ALU = mybir.AluOpType
+ACT = mybir.ActivationFunctionType
+
+K, T, S, V, H = 512, 1024, 512, 256, 512
+P = 128
+PACK = 4
+N = 128
+FLOPS = 2 * K * H * S + 2 * H * H * V
+
+
+def tile_picked_siam_abs_po_kernel(tc, x_words, x_scales, w1, w2_words, w2_scales, offs, out_0, out_1, out_2):
+    nc = tc.nc
+    with ExitStack() as ctx:
+        keep = ctx.enter_context(tc.tile_pool(name="keep", bufs=1))
+        psum = ctx.enter_context(tc.psum_pool(name="psum", bufs=1))
+
+        def sb(shape, dtype, name):
+            return keep.tile(shape, dtype, name=name, align_bytes=64)
+
+        offsets = sb([P, S // 16], U16, "offsets")
+        xw = sb([P, T], U32, "xw")
+        xs = sb([P, T], U8, "xs")
+        w2w = sb([P, 2 * H], U8, "w2w")
+        w2s = sb([P, H], U8, "w2s")
+
+        nc.vector.memset(xs[:].bitcast(I32), 0)
+        nc.vector.memset(w2s[:].bitcast(I32), 0)
+
+        nc.sync.dma_start(offsets[:], offs)
+        nc.sync.dma_start(xw[:].bitcast(I32), x_words[0].rearrange("p c r -> p (c r)").bitcast(I32))
+        for q in range(4):
+            nc.scalar.dma_start(xs[32 * q : 32 * q + 4, :].bitcast(I32), x_scales[0, 4 * q : 4 * q + 4, :].bitcast(I32))
+        w1v = w1.rearrange("(p j) c -> p j c", j=PACK)
+        HALF = H // 2
+        w1raw = [sb([P, PACK, HALF], F32, "w1raw%d" % h) for h in range(2)]
+        for h in range(2):
+            nc.sync.dma_start(w1raw[h][:], w1v[:, :, h * HALF : (h + 1) * HALF])
+        nc.sync.dma_start(w2w[:].bitcast(I32), w2_words[0].bitcast(I32))
+        for q in range(4):
+            nc.sync.dma_start(w2s[32 * q : 32 * q + 4, :].bitcast(I32), w2_scales[0, 4 * q : 4 * q + 4, :].bitcast(I32))
+
+        gw = sb([P, S], U32, "gw")
+        gs = sb([P, S], U8, "gs")
+        nc.vector.tensor_copy(gw[:], xw[:].indirect(offsets[:]))
+        nc.vector.tensor_copy(gs[:], xs[:].indirect(offsets[:]))
+
+        w1g = sb([P, PACK, P, PACK], BF16, "w1g")
+
+        def deal_w1(copy, h, m0, m1):
+            src = w1raw[h][:].rearrange("p j (m t) -> p m j t", t=PACK)[:, m0:m1]
+            dst = w1g[:].rearrange("p t m j -> p m j t")[:, 64 * h + m0 : 64 * h + m1]
+            copy(dst, src)
+
+        deal_w1(nc.scalar.copy, 0, 0, 64)
+        deal_w1(nc.scalar.copy, 1, 0, 20)
+        deal_w1(nc.vector.tensor_copy, 1, 20, 64)
+
+        w1c = sb([P, H], U32, "w1c")
+        w1s = sb([P, H], U8, "w1s")
+        for t in range(PACK):
+            cols = slice(t * P, (t + 1) * P)
+            nc.vector.quantize_mx(out=w1c[:, cols].bitcast(FP8X4), scales=w1s[:, cols], in_=w1g[:, t].rearrange("p m j -> p (m j)"))
+
+        w2c = sb([P, PACK, 2 * P], U8, "w2c")
+        w2d = sb([P, PACK, P], U8, "w2d")
+        nc.vector.tensor_copy(w2c[:].rearrange("p t (m b) -> p m t b", b=2), w2w[:].rearrange("p (m t b) -> p m t b", t=PACK, b=2))
+        nc.vector.tensor_copy(w2d[:].rearrange("p t m -> p m t"), w2s[:].rearrange("p (m t) -> p m t", t=PACK))
+
+        def first_layer(name, j0):
+            bank = psum.tile([P, PACK, N], F32, name=name)
+            for t in range(PACK):
+                cols = slice(t * P, (t + 1) * P)
+                nc.tensor.matmul_mx(out=bank[:, t, :], lhsT=w1c[:, cols].bitcast(FP8X4), lhsT_scale=w1s[:, cols],
+                                    rhs=gw[:, j0 : j0 + N].bitcast(FP8X4), rhs_scale=gs[:, j0 : j0 + N], start=True, stop=True)
+            return bank
+
+        chunks = range(V // N)
+        zc, zs, z = {}, {}, {}
+        for c in chunks:
+            a = first_layer("a%d" % c, c * N)
+            b = first_layer("b%d" % c, V + c * N)
+            ra = sb([P, N, PACK], F32, "ra%d" % c)
+            nc.scalar.activation(ra[:], a[:].rearrange("p t n -> p n t"), ACT.Relu)
+            d = sb([P, N, PACK], BF16, "d%d" % c)
+            nc.vector.scalar_tensor_tensor(d[:], b[:].rearrange("p t n -> p n t"), 0.0, ra[:], ALU.max, ALU.subtract)
+            z[c] = sb([P, N * PACK], BF16, "z%d" % c)
+            dd = d[:].rearrange("p n t -> p (n t)")
+            nc.vector.scalar_tensor_tensor(z[c][:], dd, -1.0, dd, ALU.mult, ALU.max)
+            zc[c] = sb([P, N], U32, "zc%d" % c)
+            zs[c] = sb([P, N], U8, "zs%d" % c)
+            nc.vector.quantize_mx(out=zc[c][:].bitcast(FP8X4), scales=zs[c][:], in_=z[c][:])
+
+        yc = sb([P, V], U32, "yc")
+        ys = sb([P, V], U8, "ys")
+        o0 = out_0.rearrange("(p t) v -> p t v", t=PACK)
+        o1 = out_1[0].rearrange("p c r -> p (c r)").bitcast(I32)
+        for c in chunks:
+            cols = slice(c * N, (c + 1) * N)
+            y = sb([P, PACK, N], F32, "y%d" % c)
+            for u in range(2):
+                bank = psum.tile([P, 2, N], F32, name="o%d%d" % (c, u))
+                for i in range(2):
+                    t = 2 * u + i
+                    nc.tensor.matmul_mx(out=bank[:, i, :], lhsT=w2c[:, t, :].bitcast(FP4X4), lhsT_scale=w2d[:, t, :],
+                                        rhs=zc[c][:].bitcast(FP8X4), rhs_scale=zs[c][:], start=True, stop=True)
+                nc.scalar.copy(y[:, 2 * u : 2 * u + 2, :], bank[:])
+            nc.sync.dma_start(o0[:, :, cols], y[:])
+            yb = sb([P, N, PACK], BF16, "yb%d" % c)
+            nc.vector.tensor_copy(yb[:].rearrange("p (n i) t -> p n t i", i=4), y[:].rearrange("p t (n i) -> p n t i", i=4))
+            nc.vector.quantize_mx(out=yc[:, cols].bitcast(FP8X4), scales=ys[:, cols], in_=yb[:].rearrange("p n t -> p (n t)"))
+            nc.sync.dma_start(o1[:, cols], yc[:, cols].bitcast(I32))
+        for q in range(4):
+            eng = nc.sync if q % 2 else nc.scalar
+            eng.dma_start(out_2[0, 4 * q : 4 * q + 4, :].bitcast(I32), ys[32 * q : 32 * q + 4, :].bitcast(I32))

@@ -26,8 +26,8 @@ def tile_picked_siam_abs_po_kernel(tc, x_words, x_scales, w1, w2_words, w2_scale
         keep = ctx.enter_context(tc.tile_pool(name="keep", bufs=1))
         psum = ctx.enter_context(tc.psum_pool(name="psum", bufs=1))
 
-        def sb(shape, dtype, name):
-            return keep.tile(shape, dtype, name=name, align_bytes=64)
+        def sb(shape, dtype, name, tag=None):
+            return keep.tile(shape, dtype, name=name, tag=tag or name, align_bytes=64)
 
         offsets = sb([P, S // 16], U16, "offsets")
         xw = sb([P, T], U32, "xw")
@@ -36,12 +36,12 @@ def tile_picked_siam_abs_po_kernel(tc, x_words, x_scales, w1, w2_words, w2_scale
         w2s = sb([P, H], U8, "w2s")
 
         nc.vector.memset(xs[:].bitcast(I32), 0)
-        nc.vector.memset(w2s[:].bitcast(I32), 0)
+        nc.gpsimd.memset(w2s[:].bitcast(I32), 0)
 
-        nc.sync.dma_start(offsets[:], offs)
         nc.sync.dma_start(xw[:].bitcast(I32), x_words[0].rearrange("p c r -> p (c r)").bitcast(I32))
+        nc.sync.dma_start(offsets[:], offs)
         for q in range(4):
-            nc.scalar.dma_start(xs[32 * q : 32 * q + 4, :].bitcast(I32), x_scales[0, 4 * q : 4 * q + 4, :].bitcast(I32))
+            nc.sync.dma_start(xs[32 * q : 32 * q + 4, :].bitcast(I32), x_scales[0, 4 * q : 4 * q + 4, :].bitcast(I32))
         w1v = w1.rearrange("(p j) c -> p j c", j=PACK)
         HALF = H // 2
         w1raw = [sb([P, PACK, HALF], F32, "w1raw%d" % h) for h in range(2)]
@@ -73,8 +73,8 @@ def tile_picked_siam_abs_po_kernel(tc, x_words, x_scales, w1, w2_words, w2_scale
             cols = slice(t * P, (t + 1) * P)
             nc.vector.quantize_mx(out=w1c[:, cols].bitcast(FP8X4), scales=w1s[:, cols], in_=w1g[:, t].rearrange("p m j -> p (m j)"))
 
-        w2c = sb([P, PACK, 2 * P], U8, "w2c")
-        w2d = sb([P, PACK, P], U8, "w2d")
+        w2c = sb([P, PACK, 2 * P], U8, "w2c", tag="w1g")
+        w2d = sb([P, PACK, P], U8, "w2d", tag="w1raw1")
         nc.vector.tensor_copy(w2c[:].rearrange("p t (m b) -> p m t b", b=2), w2w[:].rearrange("p (m t b) -> p m t b", t=PACK, b=2))
         nc.vector.tensor_copy(w2d[:].rearrange("p t m -> p m t"), w2s[:].rearrange("p (m t) -> p m t", t=PACK))
 
@@ -93,11 +93,12 @@ def tile_picked_siam_abs_po_kernel(tc, x_words, x_scales, w1, w2_words, w2_scale
             b = first_layer("b%d" % c, V + c * N)
             ra = sb([P, N, PACK], F32, "ra%d" % c)
             nc.scalar.activation(ra[:], a[:].rearrange("p t n -> p n t"), ACT.Relu)
-            d = sb([P, N, PACK], BF16, "d%d" % c)
-            nc.vector.scalar_tensor_tensor(d[:], b[:].rearrange("p t n -> p n t"), 0.0, ra[:], ALU.max, ALU.subtract)
             z[c] = sb([P, N * PACK], BF16, "z%d" % c)
-            dd = d[:].rearrange("p n t -> p (n t)")
-            nc.vector.scalar_tensor_tensor(z[c][:], dd, -1.0, dd, ALU.mult, ALU.max)
+            for e in range(2):
+                ns = slice(e * N // 2, (e + 1) * N // 2)
+                d = sb([P, N // 2, PACK], F32, "d%d%d" % (c, e))
+                nc.vector.scalar_tensor_tensor(d[:], b[:].rearrange("p t n -> p n t")[:, ns], 0.0, ra[:, ns], ALU.max, ALU.subtract)
+                nc.scalar.activation(z[c][:, e * 2 * N : (e + 1) * 2 * N], d[:].rearrange("p n t -> p (n t)"), ACT.Abs)
             zc[c] = sb([P, N], U32, "zc%d" % c)
             zs[c] = sb([P, N], U8, "zs%d" % c)
             nc.vector.quantize_mx(out=zc[c][:].bitcast(FP8X4), scales=zs[c][:], in_=z[c][:])

@@ -52,9 +52,9 @@ def tile_picked_siam_abs_po_kernel(tc, x_words, x_scales, w1, w2_words, w2_scale
             nc.sync.dma_start(w2s[32 * q : 32 * q + 4, :].bitcast(I32), w2_scales[0, 4 * q : 4 * q + 4, :].bitcast(I32))
 
         gw = sb([P, S], U32, "gw")
-        gs = sb([P, S], U8, "gs")
+        gs = [sb([P, V], U8, "gs0")]
         nc.vector.tensor_copy(gw[:], xw[:].indirect(offsets[:]))
-        nc.vector.tensor_copy(gs[:], xs[:].indirect(offsets[:]))
+        nc.vector.tensor_copy(gs[0][:], xs[:].indirect(offsets[:, : V // 16]))
 
         w1g = sb([P, PACK, P, PACK], BF16, "w1g")
 
@@ -63,7 +63,8 @@ def tile_picked_siam_abs_po_kernel(tc, x_words, x_scales, w1, w2_words, w2_scale
             dst = w1g[:].rearrange("p t m j -> p m j t")[:, 64 * h + m0 : 64 * h + m1]
             copy(dst, src)
 
-        deal_w1(nc.scalar.copy, 0, 0, 64)
+        deal_w1(nc.scalar.copy, 0, 0, 48)
+        deal_w1(nc.vector.tensor_copy, 0, 48, 64)
         deal_w1(nc.scalar.copy, 1, 0, 20)
         deal_w1(nc.vector.tensor_copy, 1, 20, 64)
 
@@ -73,24 +74,31 @@ def tile_picked_siam_abs_po_kernel(tc, x_words, x_scales, w1, w2_words, w2_scale
             cols = slice(t * P, (t + 1) * P)
             nc.vector.quantize_mx(out=w1c[:, cols].bitcast(FP8X4), scales=w1s[:, cols], in_=w1g[:, t].rearrange("p m j -> p (m j)"))
 
-        w2c = sb([P, PACK, 2 * P], U8, "w2c", tag="w1g")
-        w2d = sb([P, PACK, P], U8, "w2d", tag="w1raw1")
+        gs.append(sb([P, V], U8, "gs1", tag="w1raw1"))
+        nc.vector.tensor_copy(gs[1][:], xs[:].indirect(offsets[:, V // 16 :]))
+
+        w2c = sb([P, PACK, 2 * P], U8, "w2c", tag="xs")
+        w2d = sb([P, PACK, P], U8, "w2d", tag="w1g")
         nc.vector.tensor_copy(w2c[:].rearrange("p t (m b) -> p m t b", b=2), w2w[:].rearrange("p (m t b) -> p m t b", t=PACK, b=2))
         nc.vector.tensor_copy(w2d[:].rearrange("p t m -> p m t"), w2s[:].rearrange("p (m t) -> p m t", t=PACK))
 
-        def first_layer(name, j0):
-            bank = psum.tile([P, PACK, N], F32, name=name)
-            for t in range(PACK):
-                cols = slice(t * P, (t + 1) * P)
-                nc.tensor.matmul_mx(out=bank[:, t, :], lhsT=w1c[:, cols].bitcast(FP8X4), lhsT_scale=w1s[:, cols],
-                                    rhs=gw[:, j0 : j0 + N].bitcast(FP8X4), rhs_scale=gs[:, j0 : j0 + N], start=True, stop=True)
-            return bank
-
         chunks = range(V // N)
+        first = {(side, c): psum.tile([P, PACK, N], F32, name="h%d%d" % (side, c)) for side in range(2) for c in chunks}
+
+        def first_layer(side, c, t):
+            cols = slice(t * P, (t + 1) * P)
+            j0 = side * V + c * N
+            nc.tensor.matmul_mx(out=first[side, c][:, t, :], lhsT=w1c[:, cols].bitcast(FP8X4), lhsT_scale=w1s[:, cols],
+                                rhs=gw[:, j0 : j0 + N].bitcast(FP8X4), rhs_scale=gs[side][:, c * N : (c + 1) * N], start=True, stop=True)
+
+        for side in range(2):
+            for c in chunks:
+                for t in range(PACK):
+                    first_layer(side, c, t)
+
         zc, zs, z = {}, {}, {}
         for c in chunks:
-            a = first_layer("a%d" % c, c * N)
-            b = first_layer("b%d" % c, V + c * N)
+            a, b = first[0, c], first[1, c]
             ra = sb([P, N, PACK], F32, "ra%d" % c)
             nc.scalar.activation(ra[:], a[:].rearrange("p t n -> p n t"), ACT.Relu)
             z[c] = sb([P, N * PACK], BF16, "z%d" % c)
@@ -110,16 +118,16 @@ def tile_picked_siam_abs_po_kernel(tc, x_words, x_scales, w1, w2_words, w2_scale
         for c in chunks:
             cols = slice(c * N, (c + 1) * N)
             y = sb([P, PACK, N], F32, "y%d" % c)
-            for u in range(2):
-                bank = psum.tile([P, 2, N], F32, name="o%d%d" % (c, u))
-                for i in range(2):
-                    t = 2 * u + i
-                    nc.tensor.matmul_mx(out=bank[:, i, :], lhsT=w2c[:, t, :].bitcast(FP4X4), lhsT_scale=w2d[:, t, :],
-                                        rhs=zc[c][:].bitcast(FP8X4), rhs_scale=zs[c][:], start=True, stop=True)
-                nc.scalar.copy(y[:, 2 * u : 2 * u + 2, :], bank[:])
-            nc.sync.dma_start(o0[:, :, cols], y[:])
             yb = sb([P, N, PACK], BF16, "yb%d" % c)
-            nc.vector.tensor_copy(yb[:].rearrange("p (n i) t -> p n t i", i=4), y[:].rearrange("p t (n i) -> p n t i", i=4))
+            for t in range(PACK):
+                bank = psum.tile([P, N], F32, name="o%d%d" % (c, t), tag=("o%d" % t if c == 0 else "h%d%d" % divmod(t, 2)))
+                nc.tensor.matmul_mx(out=bank[:], lhsT=w2c[:, t, :].bitcast(FP4X4), lhsT_scale=w2d[:, t, :],
+                                    rhs=zc[c][:].bitcast(FP8X4), rhs_scale=zs[c][:], start=True, stop=True)
+                nc.scalar.copy(y[:, t, :], bank[:])
+                if t % 2:
+                    nc.vector.tensor_copy(yb[:, :, t - 1 : t + 1].rearrange("p (n i) t -> p n t i", i=4),
+                                          y[:, t - 1 : t + 1, :].rearrange("p t (n i) -> p n t i", i=4))
+            nc.sync.dma_start(o0[:, :, cols], y[:])
             nc.vector.quantize_mx(out=yc[:, cols].bitcast(FP8X4), scales=ys[:, cols], in_=yb[:].rearrange("p n t -> p (n t)"))
             nc.sync.dma_start(o1[:, cols], yc[:, cols].bitcast(I32))
         for q in range(4):

@@ -56,6 +56,11 @@ def tile_picked_siam_abs_po_kernel(tc, x_words, x_scales, w1, w2_words, w2_scale
         nc.vector.tensor_copy(gw[:], xw[:].indirect(offsets[:]))
         nc.vector.tensor_copy(gs[0][:], xs[:].indirect(offsets[:, : V // 16]))
 
+        for i in range(3):
+            warm = psum.tile([P, V], F32, name="warm%d" % i, tag="o%d" % i)
+            nc.tensor.matmul_mx(out=warm[:], lhsT=gw[:, :P].bitcast(FP8X4), lhsT_scale=gs[0][:, :P],
+                                rhs=gw[:, :V].bitcast(FP8X4), rhs_scale=gs[0][:], start=True, stop=True)
+
         w1g = sb([P, PACK, P, PACK], BF16, "w1g")
 
         def deal_w1(copy, h, m0, m1):

@@ -17,6 +17,7 @@ K, T, S, V, H = 512, 1024, 512, 256, 512
 P = 128
 PACK = 4
 N = 128
+SCALAR_PLACES = (48, 28)
 FLOPS = 2 * K * H * S + 2 * H * H * V
 
 
@@ -32,60 +33,58 @@ def tile_picked_siam_abs_po_kernel(tc, x_words, x_scales, w1, w2_words, w2_scale
         offsets = sb([P, S // 16], U16, "offsets")
         xw = sb([P, T], U32, "xw")
         xs = sb([P, T], U8, "xs")
-        w2w = sb([P, 2 * H], U8, "w2w")
         w2s = sb([P, H], U8, "w2s")
 
         nc.vector.memset(xs[:].bitcast(I32), 0)
         nc.gpsimd.memset(w2s[:].bitcast(I32), 0)
 
-        nc.sync.dma_start(xw[:].bitcast(I32), x_words[0].rearrange("p c r -> p (c r)").bitcast(I32))
+        xv = x_words[0].rearrange("p c r -> p (c r)").bitcast(I32)
+        nc.sync.dma_start(xw[:, : T // 2].bitcast(I32), xv[:, : T // 2])
         nc.sync.dma_start(offsets[:], offs)
         for q in range(4):
             nc.sync.dma_start(xs[32 * q : 32 * q + 4, :].bitcast(I32), x_scales[0, 4 * q : 4 * q + 4, :].bitcast(I32))
+        nc.sync.dma_start(xw[:, T // 2 :].bitcast(I32), xv[:, T // 2 :])
         w1v = w1.rearrange("(p j) c -> p j c", j=PACK)
         HALF = H // 2
         w1raw = [sb([P, PACK, HALF], F32, "w1raw%d" % h) for h in range(2)]
         for h in range(2):
             nc.sync.dma_start(w1raw[h][:], w1v[:, :, h * HALF : (h + 1) * HALF])
+        w2w = sb([P, 2 * H], U8, "w2w")
         nc.sync.dma_start(w2w[:].bitcast(I32), w2_words[0].bitcast(I32))
         for q in range(4):
             nc.sync.dma_start(w2s[32 * q : 32 * q + 4, :].bitcast(I32), w2_scales[0, 4 * q : 4 * q + 4, :].bitcast(I32))
 
         gw = sb([P, S], U32, "gw")
-        gs = [sb([P, V], U8, "gs0")]
+        gs = sb([P, S], U8, "gs")
+        nc.vector.tensor_copy(gs[:], xs[:].indirect(offsets[:]))
         nc.vector.tensor_copy(gw[:], xw[:].indirect(offsets[:]))
-        nc.vector.tensor_copy(gs[0][:], xs[:].indirect(offsets[:, : V // 16]))
 
-        for i in range(3):
-            warm = psum.tile([P, V], F32, name="warm%d" % i, tag="o%d" % i)
-            nc.tensor.matmul_mx(out=warm[:], lhsT=gw[:, :P].bitcast(FP8X4), lhsT_scale=gs[0][:, :P],
-                                rhs=gw[:, :V].bitcast(FP8X4), rhs_scale=gs[0][:], start=True, stop=True)
+        for i in range(2):
+            warm = psum.tile([P // 2, S], F32, name="warm%d" % i, tag="o%d" % i)
+            nc.tensor.matmul_mx(out=warm[:], lhsT=gw[:, : P // 2].bitcast(FP8X4), lhsT_scale=gs[:, : P // 2],
+                                rhs=gw[:].bitcast(FP8X4), rhs_scale=gs[:], start=True, stop=True)
 
-        w1g = sb([P, PACK, P, PACK], BF16, "w1g")
+        M = P // 2
+        w1g = [sb([P, PACK, M, PACK], BF16, "w1g%d" % h) for h in range(2)]
+        w1c = sb([P, H], U32, "w1c")
+        w1s = sb([P, H], U8, "w1s")
 
         def deal_w1(copy, h, m0, m1):
             src = w1raw[h][:].rearrange("p j (m t) -> p m j t", t=PACK)[:, m0:m1]
-            dst = w1g[:].rearrange("p t m j -> p m j t")[:, 64 * h + m0 : 64 * h + m1]
+            dst = w1g[h][:].rearrange("p t m j -> p m j t")[:, m0:m1]
             copy(dst, src)
 
-        deal_w1(nc.scalar.copy, 0, 0, 48)
-        deal_w1(nc.vector.tensor_copy, 0, 48, 64)
-        deal_w1(nc.scalar.copy, 1, 0, 20)
-        deal_w1(nc.vector.tensor_copy, 1, 20, 64)
+        for h in range(2):
+            deal_w1(nc.scalar.copy, h, 0, SCALAR_PLACES[h])
+            deal_w1(nc.vector.tensor_copy, h, SCALAR_PLACES[h], M)
+            for t in range(PACK):
+                cols = slice(t * P + h * M, t * P + (h + 1) * M)
+                nc.vector.quantize_mx(out=w1c[:, cols].bitcast(FP8X4), scales=w1s[:, cols], in_=w1g[h][:, t].rearrange("p m j -> p (m j)"))
 
-        w1c = sb([P, H], U32, "w1c")
-        w1s = sb([P, H], U8, "w1s")
-        for t in range(PACK):
-            cols = slice(t * P, (t + 1) * P)
-            nc.vector.quantize_mx(out=w1c[:, cols].bitcast(FP8X4), scales=w1s[:, cols], in_=w1g[:, t].rearrange("p m j -> p (m j)"))
-
-        gs.append(sb([P, V], U8, "gs1", tag="w1raw1"))
-        nc.vector.tensor_copy(gs[1][:], xs[:].indirect(offsets[:, V // 16 :]))
-
-        w2c = sb([P, PACK, 2 * P], U8, "w2c", tag="xs")
-        w2d = sb([P, PACK, P], U8, "w2d", tag="w1g")
-        nc.vector.tensor_copy(w2c[:].rearrange("p t (m b) -> p m t b", b=2), w2w[:].rearrange("p (m t b) -> p m t b", t=PACK, b=2))
+        w2d = sb([P, PACK, P], U8, "w2d", tag="w1raw1")
+        w2c = sb([P, PACK, 2 * P], U8, "w2c", tag="w1g1")
         nc.vector.tensor_copy(w2d[:].rearrange("p t m -> p m t"), w2s[:].rearrange("p (m t) -> p m t", t=PACK))
+        nc.vector.tensor_copy(w2c[:].rearrange("p t (m b) -> p m t b", b=2), w2w[:].rearrange("p (m t b) -> p m t b", t=PACK, b=2))
 
         chunks = range(V // N)
         first = {(side, c): psum.tile([P, PACK, N], F32, name="h%d%d" % (side, c)) for side in range(2) for c in chunks}
@@ -94,23 +93,23 @@ def tile_picked_siam_abs_po_kernel(tc, x_words, x_scales, w1, w2_words, w2_scale
             cols = slice(t * P, (t + 1) * P)
             j0 = side * V + c * N
             nc.tensor.matmul_mx(out=first[side, c][:, t, :], lhsT=w1c[:, cols].bitcast(FP8X4), lhsT_scale=w1s[:, cols],
-                                rhs=gw[:, j0 : j0 + N].bitcast(FP8X4), rhs_scale=gs[side][:, c * N : (c + 1) * N], start=True, stop=True)
+                                rhs=gw[:, j0 : j0 + N].bitcast(FP8X4), rhs_scale=gs[:, j0 : j0 + N], start=True, stop=True)
 
-        for side in range(2):
-            for c in chunks:
+        for c in chunks:
+            for side in range(2):
                 for t in range(PACK):
                     first_layer(side, c, t)
 
         zc, zs, z = {}, {}, {}
         for c in chunks:
             a, b = first[0, c], first[1, c]
-            ra = sb([P, N, PACK], F32, "ra%d" % c)
-            nc.scalar.activation(ra[:], a[:].rearrange("p t n -> p n t"), ACT.Relu)
             z[c] = sb([P, N * PACK], BF16, "z%d" % c)
             for e in range(2):
                 ns = slice(e * N // 2, (e + 1) * N // 2)
+                ra = sb([P, N // 2, PACK], F32, "ra%d%d" % (c, e))
+                nc.scalar.activation(ra[:], a[:].rearrange("p t n -> p n t")[:, ns], ACT.Relu)
                 d = sb([P, N // 2, PACK], F32, "d%d%d" % (c, e))
-                nc.vector.scalar_tensor_tensor(d[:], b[:].rearrange("p t n -> p n t")[:, ns], 0.0, ra[:, ns], ALU.max, ALU.subtract)
+                nc.vector.scalar_tensor_tensor(d[:], b[:].rearrange("p t n -> p n t")[:, ns], 0.0, ra[:], ALU.max, ALU.subtract)
                 nc.scalar.activation(z[c][:, e * 2 * N : (e + 1) * 2 * N], d[:].rearrange("p n t -> p (n t)"), ACT.Abs)
             zc[c] = sb([P, N], U32, "zc%d" % c)
             zs[c] = sb([P, N], U8, "zs%d" % c)
@@ -124,14 +123,16 @@ def tile_picked_siam_abs_po_kernel(tc, x_words, x_scales, w1, w2_words, w2_scale
             cols = slice(c * N, (c + 1) * N)
             y = sb([P, PACK, N], F32, "y%d" % c)
             yb = sb([P, N, PACK], BF16, "yb%d" % c)
-            for t in range(PACK):
-                bank = psum.tile([P, N], F32, name="o%d%d" % (c, t), tag=("o%d" % t if c == 0 else "h%d%d" % divmod(t, 2)))
-                nc.tensor.matmul_mx(out=bank[:], lhsT=w2c[:, t, :].bitcast(FP4X4), lhsT_scale=w2d[:, t, :],
-                                    rhs=zc[c][:].bitcast(FP8X4), rhs_scale=zs[c][:], start=True, stop=True)
-                nc.scalar.copy(y[:, t, :], bank[:])
-                if t % 2:
-                    nc.vector.tensor_copy(yb[:, :, t - 1 : t + 1].rearrange("p (n i) t -> p n t i", i=4),
-                                          y[:, t - 1 : t + 1, :].rearrange("p t (n i) -> p n t i", i=4))
+            for u in range(2):
+                bank = psum.tile([P, 2, N], F32, name="o%d%d" % (c, u), tag="o%d" % (2 * c + u))
+                for e in range(2):
+                    t = 2 * u + e
+                    nc.tensor.matmul_mx(out=bank[:, e, :], lhsT=w2c[:, t, :].bitcast(FP4X4), lhsT_scale=w2d[:, t, :],
+                                        rhs=zc[c][:].bitcast(FP8X4), rhs_scale=zs[c][:], start=True, stop=True)
+                ts = slice(2 * u, 2 * u + 2)
+                empty = nc.vector.tensor_copy if (c, u) == (1, 1) else nc.scalar.copy
+                empty(y[:, ts, :], bank[:])
+            nc.vector.tensor_copy(yb[:].rearrange("p (n i) t -> p n t i", i=4), y[:].rearrange("p t (n i) -> p n t i", i=4))
             nc.sync.dma_start(o0[:, :, cols], y[:])
             nc.vector.quantize_mx(out=yc[:, cols].bitcast(FP8X4), scales=ys[:, cols], in_=yb[:].rearrange("p n t -> p (n t)"))
             nc.sync.dma_start(o1[:, cols], yc[:, cols].bitcast(I32))

@@ -17,7 +17,8 @@ K, T, S, V, H = 512, 1024, 512, 256, 512
 P = 128
 PACK = 4
 N = 128
-SCALAR_PLACES = (48, 28)
+SCALAR_PLACES = 22
+X_FIRST = 512
 FLOPS = 2 * K * H * S + 2 * H * H * V
 
 
@@ -25,6 +26,7 @@ def tile_picked_siam_abs_po_kernel(tc, x_words, x_scales, w1, w2_words, w2_scale
     nc = tc.nc
     with ExitStack() as ctx:
         keep = ctx.enter_context(tc.tile_pool(name="keep", bufs=1))
+        reuse = ctx.enter_context(tc.tile_pool(name="reuse", bufs=1))
         psum = ctx.enter_context(tc.psum_pool(name="psum", bufs=1))
 
         def sb(shape, dtype, name, tag=None):
@@ -34,56 +36,65 @@ def tile_picked_siam_abs_po_kernel(tc, x_words, x_scales, w1, w2_words, w2_scale
         xw = sb([P, T], U32, "xw")
         xs = sb([P, T], U8, "xs")
         w2s = sb([P, H], U8, "w2s")
+        gs = sb([P, S], U8, "gs")
 
+        gw = [sb([P, S], U32, "gw0"), sb([P, S - N], U32, "gw1")]
+        w2d = sb([P, H], U8, "w2d")
         nc.vector.memset(xs[:].bitcast(I32), 0)
-        nc.gpsimd.memset(w2s[:].bitcast(I32), 0)
+        nc.vector.memset(w2s[:].bitcast(I32), 0)
+        nc.vector.memset(w2d[:].bitcast(I32), 0)
+        nc.vector.memset(gs[:].bitcast(I32), 0)
+        nc.vector.memset(gw[0][:, N:].bitcast(I32), 0)
 
         xv = x_words[0].rearrange("p c r -> p (c r)").bitcast(I32)
-        nc.sync.dma_start(xw[:, : T // 2].bitcast(I32), xv[:, : T // 2])
+        nc.sync.dma_start(xw[:, :X_FIRST].bitcast(I32), xv[:, :X_FIRST])
         nc.sync.dma_start(offsets[:], offs)
-        for q in range(4):
-            nc.sync.dma_start(xs[32 * q : 32 * q + 4, :].bitcast(I32), x_scales[0, 4 * q : 4 * q + 4, :].bitcast(I32))
-        nc.sync.dma_start(xw[:, T // 2 :].bitcast(I32), xv[:, T // 2 :])
+        nc.sync.dma_start(xs[0:P:8, :].bitcast(I32), x_scales[0].bitcast(I32))
+        nc.sync.dma_start(xw[:, X_FIRST:].bitcast(I32), xv[:, X_FIRST:])
         w1v = w1.rearrange("(p j) c -> p j c", j=PACK)
         HALF = H // 2
         w1raw = [sb([P, PACK, HALF], F32, "w1raw%d" % h) for h in range(2)]
         for h in range(2):
             nc.sync.dma_start(w1raw[h][:], w1v[:, :, h * HALF : (h + 1) * HALF])
+        nc.sync.dma_start(w2s[0:P:8, :].bitcast(I32), w2_scales[0].bitcast(I32))
         w2w = sb([P, 2 * H], U8, "w2w")
         nc.sync.dma_start(w2w[:].bitcast(I32), w2_words[0].bitcast(I32))
-        for q in range(4):
-            nc.sync.dma_start(w2s[32 * q : 32 * q + 4, :].bitcast(I32), w2_scales[0, 4 * q : 4 * q + 4, :].bitcast(I32))
 
-        gw = sb([P, S], U32, "gw")
-        gs = sb([P, S], U8, "gs")
-        nc.vector.tensor_copy(gs[:], xs[:].indirect(offsets[:]))
-        nc.vector.tensor_copy(gw[:], xw[:].indirect(offsets[:]))
+        spread = sb([P, S], U8, "spread")
+        nc.vector.tensor_copy(spread[:], xs[:].indirect(offsets[:]))
+        nc.vector.tensor_copy(gw[0][:, :N], xw[:].indirect(offsets[:, : N // 16]))
+        nc.vector.tensor_copy(gw[1][:], xw[:].indirect(offsets[:, N // 16 :]))
+        for q in range(4):
+            nc.sync.dma_start(gs[32 * q : 32 * q + 4, :].bitcast(I32), spread[32 * q : 32 * q + 32 : 8, :].bitcast(I32))
 
         for i in range(2):
             warm = psum.tile([P // 2, S], F32, name="warm%d" % i, tag="o%d" % i)
-            nc.tensor.matmul_mx(out=warm[:], lhsT=gw[:, : P // 2].bitcast(FP8X4), lhsT_scale=gs[:, : P // 2],
-                                rhs=gw[:].bitcast(FP8X4), rhs_scale=gs[:], start=True, stop=True)
+            nc.tensor.matmul_mx(out=warm[:], lhsT=gw[0][:, : P // 2].bitcast(FP8X4), lhsT_scale=spread[:, : P // 2],
+                                rhs=gw[0][:].bitcast(FP8X4), rhs_scale=spread[:], start=True, stop=True)
 
         M = P // 2
-        w1g = [sb([P, PACK, M, PACK], BF16, "w1g%d" % h) for h in range(2)]
+        w1g = reuse.tile([P, PACK, P, PACK], BF16, name="w1g", offset=0, align_bytes=64)
         w1c = sb([P, H], U32, "w1c")
         w1s = sb([P, H], U8, "w1s")
 
         def deal_w1(copy, h, m0, m1):
             src = w1raw[h][:].rearrange("p j (m t) -> p m j t", t=PACK)[:, m0:m1]
-            dst = w1g[h][:].rearrange("p t m j -> p m j t")[:, m0:m1]
+            dst = w1g[:].rearrange("p t m j -> p m j t")[:, h * M + m0 : h * M + m1]
             copy(dst, src)
 
-        for h in range(2):
-            deal_w1(nc.scalar.copy, h, 0, SCALAR_PLACES[h])
-            deal_w1(nc.vector.tensor_copy, h, SCALAR_PLACES[h], M)
-            for t in range(PACK):
-                cols = slice(t * P + h * M, t * P + (h + 1) * M)
-                nc.vector.quantize_mx(out=w1c[:, cols].bitcast(FP8X4), scales=w1s[:, cols], in_=w1g[h][:, t].rearrange("p m j -> p (m j)"))
+        deal_w1(nc.scalar.copy, 0, 0, M)
+        deal_w1(nc.scalar.copy, 1, 0, SCALAR_PLACES)
+        deal_w1(nc.vector.tensor_copy, 1, SCALAR_PLACES, M)
+        for t in range(PACK):
+            cols = slice(t * P, (t + 1) * P)
+            nc.vector.quantize_mx(out=w1c[:, cols].bitcast(FP8X4), scales=w1s[:, cols], in_=w1g[:, t].rearrange("p m j -> p (m j)"))
 
-        w2d = sb([P, PACK, P], U8, "w2d", tag="w1raw1")
-        w2c = sb([P, PACK, 2 * P], U8, "w2c", tag="w1g1")
-        nc.vector.tensor_copy(w2d[:].rearrange("p t m -> p m t"), w2s[:].rearrange("p (m t) -> p m t", t=PACK))
+        dealt = reuse.tile([P, PACK, P], U8, name="dealt", offset=0, align_bytes=64)
+        nc.vector.tensor_copy(dealt[:].rearrange("p t m -> p m t"), w2s[:].rearrange("p (m t) -> p m t", t=PACK))
+        for q in range(4):
+            nc.sync.dma_start(w2d[32 * q : 32 * q + 4, :].bitcast(I32),
+                              dealt[32 * q : 32 * q + 32 : 8].rearrange("p t m -> p (t m)").bitcast(I32))
+        w2c = reuse.tile([P, PACK, 2 * P], U8, name="w2c", offset=H, align_bytes=64)
         nc.vector.tensor_copy(w2c[:].rearrange("p t (m b) -> p m t b", b=2), w2w[:].rearrange("p (m t b) -> p m t b", t=PACK, b=2))
 
         chunks = range(V // N)
@@ -93,7 +104,7 @@ def tile_picked_siam_abs_po_kernel(tc, x_words, x_scales, w1, w2_words, w2_scale
             cols = slice(t * P, (t + 1) * P)
             j0 = side * V + c * N
             nc.tensor.matmul_mx(out=first[side, c][:, t, :], lhsT=w1c[:, cols].bitcast(FP8X4), lhsT_scale=w1s[:, cols],
-                                rhs=gw[:, j0 : j0 + N].bitcast(FP8X4), rhs_scale=gs[:, j0 : j0 + N], start=True, stop=True)
+                                rhs=(gw[1][:, j0 - N : j0] if j0 else gw[0][:, :N]).bitcast(FP8X4), rhs_scale=gs[:, j0 : j0 + N], start=True, stop=True)
 
         for c in chunks:
             for side in range(2):
@@ -127,7 +138,7 @@ def tile_picked_siam_abs_po_kernel(tc, x_words, x_scales, w1, w2_words, w2_scale
                 bank = psum.tile([P, 2, N], F32, name="o%d%d" % (c, u), tag="o%d" % (2 * c + u))
                 for e in range(2):
                     t = 2 * u + e
-                    nc.tensor.matmul_mx(out=bank[:, e, :], lhsT=w2c[:, t, :].bitcast(FP4X4), lhsT_scale=w2d[:, t, :],
+                    nc.tensor.matmul_mx(out=bank[:, e, :], lhsT=w2c[:, t, :].bitcast(FP4X4), lhsT_scale=w2d[:, t * P : (t + 1) * P],
                                         rhs=zc[c][:].bitcast(FP8X4), rhs_scale=zs[c][:], start=True, stop=True)
                 ts = slice(2 * u, 2 * u + 2)
                 empty = nc.vector.tensor_copy if (c, u) == (1, 1) else nc.scalar.copy

@@ -17,7 +17,7 @@ K, T, S, V, H = 512, 1024, 512, 256, 512
 P = 128
 PACK = 4
 N = 128
-SCALAR_PLACES = 22
+SCALAR_PLACES = 28
 X_FIRST = 512
 FLOPS = 2 * K * H * S + 2 * H * H * V
 
@@ -38,13 +38,12 @@ def tile_picked_siam_abs_po_kernel(tc, x_words, x_scales, w1, w2_words, w2_scale
         w2s = sb([P, H], U8, "w2s")
         gs = sb([P, S], U8, "gs")
 
-        gw = [sb([P, S], U32, "gw0"), sb([P, S - N], U32, "gw1")]
+        gw = sb([P, S], U32, "gw")
         w2d = sb([P, H], U8, "w2d")
         nc.vector.memset(xs[:].bitcast(I32), 0)
         nc.vector.memset(w2s[:].bitcast(I32), 0)
         nc.vector.memset(w2d[:].bitcast(I32), 0)
         nc.vector.memset(gs[:].bitcast(I32), 0)
-        nc.vector.memset(gw[0][:, N:].bitcast(I32), 0)
 
         xv = x_words[0].rearrange("p c r -> p (c r)").bitcast(I32)
         nc.sync.dma_start(xw[:, :X_FIRST].bitcast(I32), xv[:, :X_FIRST])
@@ -62,15 +61,14 @@ def tile_picked_siam_abs_po_kernel(tc, x_words, x_scales, w1, w2_words, w2_scale
 
         spread = sb([P, S], U8, "spread")
         nc.vector.tensor_copy(spread[:], xs[:].indirect(offsets[:]))
-        nc.vector.tensor_copy(gw[0][:, :N], xw[:].indirect(offsets[:, : N // 16]))
-        nc.vector.tensor_copy(gw[1][:], xw[:].indirect(offsets[:, N // 16 :]))
+        nc.vector.tensor_copy(gw[:], xw[:].indirect(offsets[:]))
         for q in range(4):
             nc.sync.dma_start(gs[32 * q : 32 * q + 4, :].bitcast(I32), spread[32 * q : 32 * q + 32 : 8, :].bitcast(I32))
 
         for i in range(2):
             warm = psum.tile([P // 2, S], F32, name="warm%d" % i, tag="o%d" % i)
-            nc.tensor.matmul_mx(out=warm[:], lhsT=gw[0][:, : P // 2].bitcast(FP8X4), lhsT_scale=spread[:, : P // 2],
-                                rhs=gw[0][:].bitcast(FP8X4), rhs_scale=spread[:], start=True, stop=True)
+            nc.tensor.matmul_mx(out=warm[:], lhsT=gw[:, : P // 2].bitcast(FP8X4), lhsT_scale=spread[:, : P // 2],
+                                rhs=gw[:].bitcast(FP8X4), rhs_scale=spread[:], start=True, stop=True)
 
         M = P // 2
         w1g = reuse.tile([P, PACK, P, PACK], BF16, name="w1g", offset=0, align_bytes=64)
@@ -85,17 +83,17 @@ def tile_picked_siam_abs_po_kernel(tc, x_words, x_scales, w1, w2_words, w2_scale
         deal_w1(nc.scalar.copy, 0, 0, M)
         deal_w1(nc.scalar.copy, 1, 0, SCALAR_PLACES)
         deal_w1(nc.vector.tensor_copy, 1, SCALAR_PLACES, M)
-        for t in range(PACK):
-            cols = slice(t * P, (t + 1) * P)
-            nc.vector.quantize_mx(out=w1c[:, cols].bitcast(FP8X4), scales=w1s[:, cols], in_=w1g[:, t].rearrange("p m j -> p (m j)"))
-
-        dealt = reuse.tile([P, PACK, P], U8, name="dealt", offset=0, align_bytes=64)
+        dealt = sb([P, PACK, P], U8, "dealt")
         nc.vector.tensor_copy(dealt[:].rearrange("p t m -> p m t"), w2s[:].rearrange("p (m t) -> p m t", t=PACK))
         for q in range(4):
             nc.sync.dma_start(w2d[32 * q : 32 * q + 4, :].bitcast(I32),
                               dealt[32 * q : 32 * q + 32 : 8].rearrange("p t m -> p (t m)").bitcast(I32))
+        for t in range(PACK):
+            cols = slice(t * P, (t + 1) * P)
+            nc.vector.quantize_mx(out=w1c[:, cols].bitcast(FP8X4), scales=w1s[:, cols], in_=w1g[:, t].rearrange("p m j -> p (m j)"))
+
         w2c = reuse.tile([P, PACK, 2 * P], U8, name="w2c", offset=H, align_bytes=64)
-        nc.vector.tensor_copy(w2c[:].rearrange("p t (m b) -> p m t b", b=2), w2w[:].rearrange("p (m t b) -> p m t b", t=PACK, b=2))
+        nc.vector.tensor_copy(w2c[:].bitcast(U16).rearrange("p t m -> p m t"), w2w[:].bitcast(U16).rearrange("p (m t) -> p m t", t=PACK))
 
         chunks = range(V // N)
         first = {(side, c): psum.tile([P, PACK, N], F32, name="h%d%d" % (side, c)) for side in range(2) for c in chunks}
@@ -104,7 +102,7 @@ def tile_picked_siam_abs_po_kernel(tc, x_words, x_scales, w1, w2_words, w2_scale
             cols = slice(t * P, (t + 1) * P)
             j0 = side * V + c * N
             nc.tensor.matmul_mx(out=first[side, c][:, t, :], lhsT=w1c[:, cols].bitcast(FP8X4), lhsT_scale=w1s[:, cols],
-                                rhs=(gw[1][:, j0 - N : j0] if j0 else gw[0][:, :N]).bitcast(FP8X4), rhs_scale=gs[:, j0 : j0 + N], start=True, stop=True)
+                                rhs=gw[:, j0 : j0 + N].bitcast(FP8X4), rhs_scale=gs[:, j0 : j0 + N], start=True, stop=True)
 
         for c in chunks:
             for side in range(2):
@@ -141,12 +139,20 @@ def tile_picked_siam_abs_po_kernel(tc, x_words, x_scales, w1, w2_words, w2_scale
                     nc.tensor.matmul_mx(out=bank[:, e, :], lhsT=w2c[:, t, :].bitcast(FP4X4), lhsT_scale=w2d[:, t * P : (t + 1) * P],
                                         rhs=zc[c][:].bitcast(FP8X4), rhs_scale=zs[c][:], start=True, stop=True)
                 ts = slice(2 * u, 2 * u + 2)
-                empty = nc.vector.tensor_copy if (c, u) == (1, 1) else nc.scalar.copy
+                empty = nc.vector.tensor_copy if (c, u) == (0, 0) else nc.scalar.copy
                 empty(y[:, ts, :], bank[:])
-            nc.vector.tensor_copy(yb[:].rearrange("p (n i) t -> p n t i", i=4), y[:].rearrange("p t (n i) -> p n t i", i=4))
-            nc.sync.dma_start(o0[:, :, cols], y[:])
-            nc.vector.quantize_mx(out=yc[:, cols].bitcast(FP8X4), scales=ys[:, cols], in_=yb[:].rearrange("p n t -> p (n t)"))
-            nc.sync.dma_start(o1[:, cols], yc[:, cols].bitcast(I32))
+                if c == 0:
+                    nc.sync.dma_start(o0[:, ts, cols], y[:, ts, :])
+            if c == 1:
+                nc.sync.dma_start(o0[:, :, cols], y[:])
+            width = N // (c + 1)
+            parts = [slice(n0, n0 + width) for n0 in range(0, N, width)]
+            for ns in parts:
+                nc.vector.tensor_copy(yb[:, ns].rearrange("p (n i) t -> p n t i", i=4), y[:, :, ns].rearrange("p t (n i) -> p n t i", i=4))
+            for ns in parts:
+                to = slice(c * N + ns.start, c * N + ns.stop)
+                nc.vector.quantize_mx(out=yc[:, to].bitcast(FP8X4), scales=ys[:, to], in_=yb[:, ns].rearrange("p n t -> p (n t)"))
+        nc.sync.dma_start(o1, yc[:].bitcast(I32))
         for q in range(4):
             eng = nc.sync if q % 2 else nc.scalar
             eng.dma_start(out_2[0, 4 * q : 4 * q + 4, :].bitcast(I32), ys[32 * q : 32 * q + 4, :].bitcast(I32))

@@ -104,10 +104,12 @@ def tile_picked_siam_abs_po_kernel(tc, x_words, x_scales, w1, w2_words, w2_scale
             nc.tensor.matmul_mx(out=first[side, c][:, t, :], lhsT=w1c[:, cols].bitcast(FP8X4), lhsT_scale=w1s[:, cols],
                                 rhs=gw[:, j0 : j0 + N].bitcast(FP8X4), rhs_scale=gs[:, j0 : j0 + N], start=True, stop=True)
 
-        for c in chunks:
+        for t in range(PACK):
             for side in range(2):
-                for t in range(PACK):
-                    first_layer(side, c, t)
+                first_layer(side, 0, t)
+        for side in range(2):
+            for t in reversed(range(PACK)):
+                first_layer(side, 1, t)
 
         zc, zs, z = {}, {}, {}
         for c in chunks:

@@ -17,7 +17,7 @@ K, T, S, V, H = 512, 1024, 512, 256, 512
 P = 128
 PACK = 4
 N = 128
-SCALAR_PLACES = 28
+SCALAR_PLACES = 34
 X_FIRST = 512
 FLOPS = 2 * K * H * S + 2 * H * H * V
 
@@ -49,15 +49,13 @@ def tile_picked_siam_abs_po_kernel(tc, x_words, x_scales, w1, w2_words, w2_scale
         nc.sync.dma_start(xw[:, :X_FIRST].bitcast(I32), xv[:, :X_FIRST])
         nc.sync.dma_start(offsets[:], offs)
         nc.sync.dma_start(xs[0:P:8, :].bitcast(I32), x_scales[0].bitcast(I32))
+        nc.sync.dma_start(w2s[0:P:8, :].bitcast(I32), w2_scales[0].bitcast(I32))
         nc.sync.dma_start(xw[:, X_FIRST:].bitcast(I32), xv[:, X_FIRST:])
         w1v = w1.rearrange("(p j) c -> p j c", j=PACK)
         HALF = H // 2
         w1raw = [sb([P, PACK, HALF], F32, "w1raw%d" % h) for h in range(2)]
         for h in range(2):
             nc.sync.dma_start(w1raw[h][:], w1v[:, :, h * HALF : (h + 1) * HALF])
-        nc.sync.dma_start(w2s[0:P:8, :].bitcast(I32), w2_scales[0].bitcast(I32))
-        w2w = sb([P, 2 * H], U8, "w2w")
-        nc.sync.dma_start(w2w[:].bitcast(I32), w2_words[0].bitcast(I32))
 
         spread = sb([P, S], U8, "spread")
         nc.vector.tensor_copy(spread[:], xs[:].indirect(offsets[:]))
@@ -65,9 +63,17 @@ def tile_picked_siam_abs_po_kernel(tc, x_words, x_scales, w1, w2_words, w2_scale
         for q in range(4):
             nc.sync.dma_start(gs[32 * q : 32 * q + 4, :].bitcast(I32), spread[32 * q : 32 * q + 32 : 8, :].bitcast(I32))
 
+        w2w = sb([P, 2 * H], U8, "w2w")
+        nc.sync.dma_start(w2w[:].bitcast(I32), w2_words[0].bitcast(I32))
+        dealt = sb([P, PACK, P], U8, "dealt")
+        nc.vector.tensor_copy(dealt[:].rearrange("p t m -> p m t"), w2s[:].rearrange("p (m t) -> p m t", t=PACK))
+        for q in range(4):
+            nc.sync.dma_start(w2d[32 * q : 32 * q + 4, :].bitcast(I32),
+                              dealt[32 * q : 32 * q + 32 : 8].rearrange("p t m -> p (t m)").bitcast(I32))
+
         for i in range(2):
-            warm = psum.tile([P // 2, S], F32, name="warm%d" % i, tag="o%d" % i)
-            nc.tensor.matmul_mx(out=warm[:], lhsT=gw[:, : P // 2].bitcast(FP8X4), lhsT_scale=spread[:, : P // 2],
+            warm = psum.tile([P // 4, S], F32, name="warm%d" % i, tag="o%d" % i)
+            nc.tensor.matmul_mx(out=warm[:], lhsT=gw[:, : P // 4].bitcast(FP8X4), lhsT_scale=spread[:, : P // 4],
                                 rhs=gw[:].bitcast(FP8X4), rhs_scale=spread[:], start=True, stop=True)
 
         M = P // 2
@@ -80,17 +86,18 @@ def tile_picked_siam_abs_po_kernel(tc, x_words, x_scales, w1, w2_words, w2_scale
             dst = w1g[:].rearrange("p t m j -> p m j t")[:, h * M + m0 : h * M + m1]
             copy(dst, src)
 
+        def quantise_w1(h, t):
+            cols = slice(t * P + h * M, t * P + (h + 1) * M)
+            nc.vector.quantize_mx(out=w1c[:, cols].bitcast(FP8X4), scales=w1s[:, cols],
+                                  in_=w1g[:, t, h * M : (h + 1) * M].rearrange("p m j -> p (m j)"))
+
         deal_w1(nc.scalar.copy, 0, 0, M)
+        for t in range(PACK):
+            quantise_w1(0, t)
         deal_w1(nc.scalar.copy, 1, 0, SCALAR_PLACES)
         deal_w1(nc.vector.tensor_copy, 1, SCALAR_PLACES, M)
-        dealt = sb([P, PACK, P], U8, "dealt")
-        nc.vector.tensor_copy(dealt[:].rearrange("p t m -> p m t"), w2s[:].rearrange("p (m t) -> p m t", t=PACK))
-        for q in range(4):
-            nc.sync.dma_start(w2d[32 * q : 32 * q + 4, :].bitcast(I32),
-                              dealt[32 * q : 32 * q + 32 : 8].rearrange("p t m -> p (t m)").bitcast(I32))
         for t in range(PACK):
-            cols = slice(t * P, (t + 1) * P)
-            nc.vector.quantize_mx(out=w1c[:, cols].bitcast(FP8X4), scales=w1s[:, cols], in_=w1g[:, t].rearrange("p m j -> p (m j)"))
+            quantise_w1(1, t)
 
         w2c = reuse.tile([P, PACK, 2 * P], U8, name="w2c", offset=H, align_bytes=64)
         nc.vector.tensor_copy(w2c[:].bitcast(U16).rearrange("p t m -> p m t"), w2w[:].bitcast(U16).rearrange("p (m t) -> p m t", t=PACK))

@@ -16,9 +16,12 @@ ACT = mybir.ActivationFunctionType
 K, T, S, V, H = 512, 1024, 512, 256, 512
 P = 128
 PACK = 4
+QUADRANTS = 4
 N = 128
-SCALAR_PLACES = 34
-X_FIRST = 512
+HALF_N = N // 2
+HALF_M = P // 2
+SCALAR_PLACES = 28
+WARM_M = 32
 FLOPS = 2 * K * H * S + 2 * H * H * V
 
 
@@ -29,139 +32,142 @@ def tile_picked_siam_abs_po_kernel(tc, x_words, x_scales, w1, w2_words, w2_scale
         reuse = ctx.enter_context(tc.tile_pool(name="reuse", bufs=1))
         psum = ctx.enter_context(tc.psum_pool(name="psum", bufs=1))
 
-        def sb(shape, dtype, name, tag=None):
-            return keep.tile(shape, dtype, name=name, tag=tag or name, align_bytes=64)
+        def sb(shape, dtype, name):
+            return keep.tile(shape, dtype, name=name, tag=name, align_bytes=64)
 
         offsets = sb([P, S // 16], U16, "offsets")
         xw = sb([P, T], U32, "xw")
         xs = sb([P, T], U8, "xs")
         w2s = sb([P, H], U8, "w2s")
         gs = sb([P, S], U8, "gs")
-
         gw = sb([P, S], U32, "gw")
-        w2d = sb([P, H], U8, "w2d")
+
         nc.vector.memset(xs[:].bitcast(I32), 0)
         nc.vector.memset(w2s[:].bitcast(I32), 0)
-        nc.vector.memset(w2d[:].bitcast(I32), 0)
         nc.vector.memset(gs[:].bitcast(I32), 0)
 
         xv = x_words[0].rearrange("p c r -> p (c r)").bitcast(I32)
-        nc.sync.dma_start(xw[:, :X_FIRST].bitcast(I32), xv[:, :X_FIRST])
+        nc.sync.dma_start(xw[:, : T // 2].bitcast(I32), xv[:, : T // 2])
         nc.sync.dma_start(offsets[:], offs)
         nc.sync.dma_start(xs[0:P:8, :].bitcast(I32), x_scales[0].bitcast(I32))
-        nc.sync.dma_start(w2s[0:P:8, :].bitcast(I32), w2_scales[0].bitcast(I32))
-        nc.sync.dma_start(xw[:, X_FIRST:].bitcast(I32), xv[:, X_FIRST:])
+        nc.sync.dma_start(xw[:, T // 2 :].bitcast(I32), xv[:, T // 2 :])
+
+        def load_w2_scales(q):
+            nc.sync.dma_start(w2s[32 * q : 32 * q + 4, :].bitcast(I32), w2_scales[0, 4 * q : 4 * q + 4, :].bitcast(I32))
+
+        for q in (0, 2):
+            load_w2_scales(q)
         w1v = w1.rearrange("(p j) c -> p j c", j=PACK)
-        HALF = H // 2
-        w1raw = [sb([P, PACK, HALF], F32, "w1raw%d" % h) for h in range(2)]
+        w1raw = [sb([P, PACK, H // 2], F32, "w1raw%d" % h) for h in range(2)]
         for h in range(2):
-            nc.sync.dma_start(w1raw[h][:], w1v[:, :, h * HALF : (h + 1) * HALF])
+            nc.sync.dma_start(w1raw[h][:], w1v[:, :, h * H // 2 : (h + 1) * H // 2])
+        w2w = sb([P, 2 * H], U8, "w2w")
+        nc.sync.dma_start(w2w[:].bitcast(I32), w2_words[0].bitcast(I32))
+        for q in (1, 3):
+            load_w2_scales(q)
 
         spread = sb([P, S], U8, "spread")
         nc.vector.tensor_copy(spread[:], xs[:].indirect(offsets[:]))
         nc.vector.tensor_copy(gw[:], xw[:].indirect(offsets[:]))
-        for q in range(4):
+        for q in range(QUADRANTS):
             nc.sync.dma_start(gs[32 * q : 32 * q + 4, :].bitcast(I32), spread[32 * q : 32 * q + 32 : 8, :].bitcast(I32))
 
-        w2w = sb([P, 2 * H], U8, "w2w")
-        nc.sync.dma_start(w2w[:].bitcast(I32), w2_words[0].bitcast(I32))
-        dealt = sb([P, PACK, P], U8, "dealt")
-        nc.vector.tensor_copy(dealt[:].rearrange("p t m -> p m t"), w2s[:].rearrange("p (m t) -> p m t", t=PACK))
-        for q in range(4):
-            nc.sync.dma_start(w2d[32 * q : 32 * q + 4, :].bitcast(I32),
-                              dealt[32 * q : 32 * q + 32 : 8].rearrange("p t m -> p (t m)").bitcast(I32))
+        for i, width in enumerate((S, S, N)):
+            warm = psum.tile([WARM_M, width], F32, name="warm%d" % i, tag="o%d" % i)
+            nc.tensor.matmul_mx(out=warm[:], lhsT=gw[:, :WARM_M].bitcast(FP8X4), lhsT_scale=spread[:, :WARM_M],
+                                rhs=gw[:, :width].bitcast(FP8X4), rhs_scale=spread[:, :width], start=True, stop=True)
 
-        for i in range(2):
-            warm = psum.tile([P // 4, S], F32, name="warm%d" % i, tag="o%d" % i)
-            nc.tensor.matmul_mx(out=warm[:], lhsT=gw[:, : P // 4].bitcast(FP8X4), lhsT_scale=spread[:, : P // 4],
-                                rhs=gw[:].bitcast(FP8X4), rhs_scale=spread[:], start=True, stop=True)
-
-        M = P // 2
         w1g = reuse.tile([P, PACK, P, PACK], BF16, name="w1g", offset=0, align_bytes=64)
         w1c = sb([P, H], U32, "w1c")
         w1s = sb([P, H], U8, "w1s")
 
-        def deal_w1(copy, h, m0, m1):
+        def round_w1(copy, h, m0, m1):
             src = w1raw[h][:].rearrange("p j (m t) -> p m j t", t=PACK)[:, m0:m1]
-            dst = w1g[:].rearrange("p t m j -> p m j t")[:, h * M + m0 : h * M + m1]
+            dst = w1g[:].rearrange("p t m j -> p m j t")[:, h * HALF_M + m0 : h * HALF_M + m1]
             copy(dst, src)
 
         def quantise_w1(h, t):
-            cols = slice(t * P + h * M, t * P + (h + 1) * M)
+            cols = slice(t * P + h * HALF_M, t * P + (h + 1) * HALF_M)
             nc.vector.quantize_mx(out=w1c[:, cols].bitcast(FP8X4), scales=w1s[:, cols],
-                                  in_=w1g[:, t, h * M : (h + 1) * M].rearrange("p m j -> p (m j)"))
+                                  in_=w1g[:, t, h * HALF_M : (h + 1) * HALF_M].rearrange("p m j -> p (m j)"))
 
-        deal_w1(nc.scalar.copy, 0, 0, M)
+        round_w1(nc.scalar.copy, 0, 0, HALF_M)
         for t in range(PACK):
             quantise_w1(0, t)
-        deal_w1(nc.scalar.copy, 1, 0, SCALAR_PLACES)
-        deal_w1(nc.vector.tensor_copy, 1, SCALAR_PLACES, M)
+        round_w1(nc.scalar.copy, 1, 0, SCALAR_PLACES)
+        round_w1(nc.vector.tensor_copy, 1, SCALAR_PLACES, HALF_M)
         for t in range(PACK):
             quantise_w1(1, t)
 
-        w2c = reuse.tile([P, PACK, 2 * P], U8, name="w2c", offset=H, align_bytes=64)
-        nc.vector.tensor_copy(w2c[:].bitcast(U16).rearrange("p t m -> p m t"), w2w[:].bitcast(U16).rearrange("p (m t) -> p m t", t=PACK))
+        w2d = reuse.tile([P, PACK, P], U8, name="w2d", offset=0, align_bytes=64)
+        nc.vector.tensor_copy(w2d[:].rearrange("p t m -> p m t"), w2s[:].rearrange("p (m t) -> p m t", t=PACK))
+        w2c = sb([P, PACK, 2 * P], U8, "w2c")
+        nc.scalar.copy(w2c[:].bitcast(U16).rearrange("p t m -> p m t"), w2w[:].bitcast(U16).rearrange("p (m t) -> p m t", t=PACK))
 
         chunks = range(V // N)
         first = {(side, c): psum.tile([P, PACK, N], F32, name="h%d%d" % (side, c)) for side in range(2) for c in chunks}
-
-        def first_layer(side, c, t):
-            cols = slice(t * P, (t + 1) * P)
-            j0 = side * V + c * N
-            nc.tensor.matmul_mx(out=first[side, c][:, t, :], lhsT=w1c[:, cols].bitcast(FP8X4), lhsT_scale=w1s[:, cols],
-                                rhs=gw[:, j0 : j0 + N].bitcast(FP8X4), rhs_scale=gs[:, j0 : j0 + N], start=True, stop=True)
-
-        for t in range(PACK):
+        for c in chunks:
             for side in range(2):
-                first_layer(side, 0, t)
-        for side in range(2):
-            for t in reversed(range(PACK)):
-                first_layer(side, 1, t)
+                picked = slice(side * V + c * N, side * V + (c + 1) * N)
+                for t in range(PACK):
+                    cols = slice(t * P, (t + 1) * P)
+                    nc.tensor.matmul_mx(out=first[side, c][:, t, :], lhsT=w1c[:, cols].bitcast(FP8X4), lhsT_scale=w1s[:, cols],
+                                        rhs=gw[:, picked].bitcast(FP8X4), rhs_scale=gs[:, picked], start=True, stop=True)
 
-        zc, zs, z = {}, {}, {}
+        zc, zs = {}, {}
         for c in chunks:
             a, b = first[0, c], first[1, c]
-            z[c] = sb([P, N * PACK], BF16, "z%d" % c)
+            z = sb([P, N * PACK], BF16, "z%d" % c)
             for e in range(2):
-                ns = slice(e * N // 2, (e + 1) * N // 2)
-                ra = sb([P, N // 2, PACK], F32, "ra%d%d" % (c, e))
+                ns = slice(e * HALF_N, (e + 1) * HALF_N)
+                ra = sb([P, HALF_N, PACK], F32, "ra%d%d" % (c, e))
                 nc.scalar.activation(ra[:], a[:].rearrange("p t n -> p n t")[:, ns], ACT.Relu)
-                d = sb([P, N // 2, PACK], F32, "d%d%d" % (c, e))
+                d = sb([P, HALF_N, PACK], F32, "d%d%d" % (c, e))
                 nc.vector.scalar_tensor_tensor(d[:], b[:].rearrange("p t n -> p n t")[:, ns], 0.0, ra[:], ALU.max, ALU.subtract)
-                nc.scalar.activation(z[c][:, e * 2 * N : (e + 1) * 2 * N], d[:].rearrange("p n t -> p (n t)"), ACT.Abs)
+                nc.scalar.activation(z[:, ns.start * PACK : ns.stop * PACK], d[:].rearrange("p n t -> p (n t)"), ACT.Abs)
             zc[c] = sb([P, N], U32, "zc%d" % c)
             zs[c] = sb([P, N], U8, "zs%d" % c)
-            nc.vector.quantize_mx(out=zc[c][:].bitcast(FP8X4), scales=zs[c][:], in_=z[c][:])
+            step = HALF_N if c == chunks[-1] else N
+            for n0 in range(0, N, step):
+                nc.vector.quantize_mx(out=zc[c][:, n0 : n0 + step].bitcast(FP8X4), scales=zs[c][:, n0 : n0 + step],
+                                      in_=z[:, n0 * PACK : (n0 + step) * PACK])
 
         yc = sb([P, V], U32, "yc")
         ys = sb([P, V], U8, "ys")
         o0 = out_0.rearrange("(p t) v -> p t v", t=PACK)
         o1 = out_1[0].rearrange("p c r -> p (c r)").bitcast(I32)
+        yb = sb([P, V, PACK], BF16, "yb")
+        y = sb([P, PACK, V], F32, "y")
+
+        def quantise_y(n0, n1):
+            nc.vector.quantize_mx(out=yc[:, n0:n1].bitcast(FP8X4), scales=ys[:, n0:n1], in_=yb[:, n0:n1].rearrange("p n t -> p (n t)"))
+
         for c in chunks:
+            last = c == chunks[-1]
             cols = slice(c * N, (c + 1) * N)
-            y = sb([P, PACK, N], F32, "y%d" % c)
-            yb = sb([P, N, PACK], BF16, "yb%d" % c)
             for u in range(2):
                 bank = psum.tile([P, 2, N], F32, name="o%d%d" % (c, u), tag="o%d" % (2 * c + u))
                 for e in range(2):
                     t = 2 * u + e
-                    nc.tensor.matmul_mx(out=bank[:, e, :], lhsT=w2c[:, t, :].bitcast(FP4X4), lhsT_scale=w2d[:, t * P : (t + 1) * P],
+                    nc.tensor.matmul_mx(out=bank[:, e, :], lhsT=w2c[:, t, :].bitcast(FP4X4), lhsT_scale=w2d[:, t, :],
                                         rhs=zc[c][:].bitcast(FP8X4), rhs_scale=zs[c][:], start=True, stop=True)
                 ts = slice(2 * u, 2 * u + 2)
-                empty = nc.vector.tensor_copy if (c, u) == (0, 0) else nc.scalar.copy
-                empty(y[:, ts, :], bank[:])
-                if c == 0:
-                    nc.sync.dma_start(o0[:, ts, cols], y[:, ts, :])
-            if c == 1:
-                nc.sync.dma_start(o0[:, :, cols], y[:])
-            width = N // (c + 1)
-            parts = [slice(n0, n0 + width) for n0 in range(0, N, width)]
-            for ns in parts:
-                nc.vector.tensor_copy(yb[:, ns].rearrange("p (n i) t -> p n t i", i=4), y[:, :, ns].rearrange("p t (n i) -> p n t i", i=4))
-            for ns in parts:
-                to = slice(c * N + ns.start, c * N + ns.stop)
-                nc.vector.quantize_mx(out=yc[:, to].bitcast(FP8X4), scales=ys[:, to], in_=yb[:, ns].rearrange("p n t -> p (n t)"))
+                empty = nc.vector.tensor_copy if last and u == 0 else nc.scalar.copy
+                empty(y[:, ts, cols], bank[:])
+                if u == 0:
+                    nc.sync.dma_start(o0[:, ts, cols], y[:, ts, cols])
+                elif last:
+                    nc.sync.dma_start(o0[:, ts, :], y[:, ts, :])
+            for e in range(2):
+                ns = slice(c * N + e * HALF_N, c * N + (e + 1) * HALF_N)
+                copy = nc.scalar.copy if last and e == 1 else nc.vector.tensor_copy
+                copy(yb[:, ns].rearrange("p (n i) t -> p n t i", i=4), y[:, :, ns].rearrange("p t (n i) -> p n t i", i=4))
+            if not last:
+                quantise_y(0, HALF_N)
+        quantise_y(V - HALF_N, V)
+        quantise_y(HALF_N, V - HALF_N)
+
         nc.sync.dma_start(o1, yc[:].bitcast(I32))
-        for q in range(4):
-            eng = nc.sync if q % 2 else nc.scalar
-            eng.dma_start(out_2[0, 4 * q : 4 * q + 4, :].bitcast(I32), ys[32 * q : 32 * q + 4, :].bitcast(I32))
+        for q in range(QUADRANTS):
+            queue = nc.sync if q % 2 else nc.scalar
+            queue.dma_start(out_2[0, 4 * q : 4 * q + 4, :].bitcast(I32), ys[32 * q : 32 * q + 4, :].bitcast(I32))

@@ -20,7 +20,8 @@ QUADRANTS = 4
 N = 128
 HALF_N = N // 2
 HALF_M = P // 2
-SCALAR_PLACES = 28
+SCALAR_PLACES = (36, 24)
+SCALAR_PAIRS = 32
 WARM_M = 32
 FLOPS = 2 * K * H * S + 2 * H * H * V
 
@@ -81,21 +82,22 @@ def tile_picked_siam_abs_po_kernel(tc, x_words, x_scales, w1, w2_words, w2_scale
         w1c = sb([P, H], U32, "w1c")
         w1s = sb([P, H], U8, "w1s")
 
-        def round_w1(copy, h, m0, m1):
-            src = w1raw[h][:].rearrange("p j (m t) -> p m j t", t=PACK)[:, m0:m1]
-            dst = w1g[:].rearrange("p t m j -> p m j t")[:, h * HALF_M + m0 : h * HALF_M + m1]
-            copy(dst, src)
+        def round_w1(h, tiles):
+            src = w1raw[h][:].rearrange("p j (m t) -> p m j t", t=PACK)[:, :, :, tiles]
+            dst = w1g[:].rearrange("p t m j -> p m j t")[:, h * HALF_M : (h + 1) * HALF_M, :, tiles]
+            nc.scalar.copy(dst[:, : SCALAR_PLACES[h]], src[:, : SCALAR_PLACES[h]])
+            nc.vector.tensor_copy(dst[:, SCALAR_PLACES[h] :], src[:, SCALAR_PLACES[h] :])
 
         def quantise_w1(h, t):
             cols = slice(t * P + h * HALF_M, t * P + (h + 1) * HALF_M)
             nc.vector.quantize_mx(out=w1c[:, cols].bitcast(FP8X4), scales=w1s[:, cols],
                                   in_=w1g[:, t, h * HALF_M : (h + 1) * HALF_M].rearrange("p m j -> p (m j)"))
 
-        round_w1(nc.scalar.copy, 0, 0, HALF_M)
+        round_w1(0, slice(0, PACK))
         for t in range(PACK):
             quantise_w1(0, t)
-        round_w1(nc.scalar.copy, 1, 0, SCALAR_PLACES)
-        round_w1(nc.vector.tensor_copy, 1, SCALAR_PLACES, HALF_M)
+        for u in range(2):
+            round_w1(1, slice(2 * u, 2 * u + 2))
         for t in range(PACK):
             quantise_w1(1, t)
 
@@ -105,7 +107,7 @@ def tile_picked_siam_abs_po_kernel(tc, x_words, x_scales, w1, w2_words, w2_scale
         nc.scalar.copy(w2c[:].bitcast(U16).rearrange("p t m -> p m t"), w2w[:].bitcast(U16).rearrange("p (m t) -> p m t", t=PACK))
 
         chunks = range(V // N)
-        first = {(side, c): psum.tile([P, PACK, N], F32, name="h%d%d" % (side, c)) for side in range(2) for c in chunks}
+        first = {(side, c): psum.tile([P, PACK, N], F32, name="h%d%d" % (side, c), tag="h%d%d" % (side, c)) for side in range(2) for c in chunks}
         for c in chunks:
             for side in range(2):
                 picked = slice(side * V + c * N, side * V + (c + 1) * N)
@@ -142,30 +144,35 @@ def tile_picked_siam_abs_po_kernel(tc, x_words, x_scales, w1, w2_words, w2_scale
         def quantise_y(n0, n1):
             nc.vector.quantize_mx(out=yc[:, n0:n1].bitcast(FP8X4), scales=ys[:, n0:n1], in_=yb[:, n0:n1].rearrange("p n t -> p (n t)"))
 
-        for c in chunks:
-            last = c == chunks[-1]
-            cols = slice(c * N, (c + 1) * N)
-            for u in range(2):
-                bank = psum.tile([P, 2, N], F32, name="o%d%d" % (c, u), tag="o%d" % (2 * c + u))
-                for e in range(2):
-                    t = 2 * u + e
-                    nc.tensor.matmul_mx(out=bank[:, e, :], lhsT=w2c[:, t, :].bitcast(FP4X4), lhsT_scale=w2d[:, t, :],
-                                        rhs=zc[c][:].bitcast(FP8X4), rhs_scale=zs[c][:], start=True, stop=True)
-                ts = slice(2 * u, 2 * u + 2)
-                empty = nc.vector.tensor_copy if last and u == 0 else nc.scalar.copy
-                empty(y[:, ts, cols], bank[:])
-                if u == 0:
-                    nc.sync.dma_start(o0[:, ts, cols], y[:, ts, cols])
-                elif last:
-                    nc.sync.dma_start(o0[:, ts, :], y[:, ts, :])
+        def product(bank, t, c):
+            nc.tensor.matmul_mx(out=bank, lhsT=w2c[:, t, :].bitcast(FP4X4), lhsT_scale=w2d[:, t, :],
+                                rhs=zc[c][:].bitcast(FP8X4), rhs_scale=zs[c][:], start=True, stop=True)
+
+        def round_y(copy, n0, n1):
+            copy(yb[:, n0:n1].rearrange("p (n i) t -> p n t i", i=4), y[:, :, n0:n1].rearrange("p t (n i) -> p n t i", i=4))
+
+        for u in range(2):
+            bank = psum.tile([P, 2, N], F32, name="o0%d" % u, tag="o%d" % u)
             for e in range(2):
-                ns = slice(c * N + e * HALF_N, c * N + (e + 1) * HALF_N)
-                copy = nc.scalar.copy if last and e == 1 else nc.vector.tensor_copy
-                copy(yb[:, ns].rearrange("p (n i) t -> p n t i", i=4), y[:, :, ns].rearrange("p t (n i) -> p n t i", i=4))
-            if not last:
-                quantise_y(0, HALF_N)
-        quantise_y(V - HALF_N, V)
-        quantise_y(HALF_N, V - HALF_N)
+                product(bank[:, e, :], 2 * u + e, 0)
+            empty = nc.scalar.copy if u else nc.vector.tensor_copy
+            empty(y[:, 2 * u : 2 * u + 2, :N], bank[:])
+        nc.sync.dma_start(o0[:, :2, :N], y[:, :2, :N])
+        round_y(nc.vector.tensor_copy, 0, N)
+        for t, tag in enumerate(("o2", "o3", "h00", "h10")):
+            bank = psum.tile([P, N], F32, name="o1%d" % t, tag=tag)
+            product(bank[:], t, 1)
+            empty = nc.scalar.copy if t % 2 else nc.vector.tensor_copy
+            empty(y[:, t, N:], bank[:])
+            if t == 1:
+                nc.sync.dma_start(o0[:, :2, N:], y[:, :2, N:])
+        nc.sync.dma_start(o0[:, 2:, :], y[:, 2:, :])
+        round_y(nc.vector.tensor_copy, N, N + HALF_N)
+        round_y(nc.vector.tensor_copy, N + HALF_N, V - SCALAR_PAIRS)
+        round_y(nc.scalar.copy, V - SCALAR_PAIRS, V)
+        quantise_y(0, N)
+        quantise_y(N, N + HALF_N)
+        quantise_y(N + HALF_N, V)
 
         nc.sync.dma_start(o1, yc[:].bitcast(I32))
         for q in range(QUADRANTS):

@@ -151,22 +151,24 @@ def tile_picked_siam_abs_po_kernel(tc, x_words, x_scales, w1, w2_words, w2_scale
         def round_y(copy, n0, n1):
             copy(yb[:, n0:n1].rearrange("p (n i) t -> p n t i", i=4), y[:, :, n0:n1].rearrange("p t (n i) -> p n t i", i=4))
 
+        y_run = y[:].rearrange("p t v -> p (t v)")
+        o_run = o0.rearrange("p t v -> p (t v)")
         for u in range(2):
             bank = psum.tile([P, 2, N], F32, name="o0%d" % u, tag="o%d" % u)
             for e in range(2):
-                product(bank[:, e, :], 2 * u + e, 0)
+                product(bank[:, e, :], u + 2 * e, 0)
             empty = nc.scalar.copy if u else nc.vector.tensor_copy
-            empty(y[:, 2 * u : 2 * u + 2, :N], bank[:])
-        nc.sync.dma_start(o0[:, :2, :N], y[:, :2, :N])
+            empty(y[:, u::2, :N], bank[:])
+        nc.sync.dma_start(o0[:, ::2, :N], y[:, ::2, :N])
         round_y(nc.vector.tensor_copy, 0, N)
         for t, tag in enumerate(("o2", "o3", "h00", "h10")):
             bank = psum.tile([P, N], F32, name="o1%d" % t, tag=tag)
             product(bank[:], t, 1)
             empty = nc.scalar.copy if t % 2 else nc.vector.tensor_copy
             empty(y[:, t, N:], bank[:])
-            if t == 1:
-                nc.sync.dma_start(o0[:, :2, N:], y[:, :2, N:])
-        nc.sync.dma_start(o0[:, 2:, :], y[:, 2:, :])
+            if t % 2:
+                run = slice((2 * t - 1) * N, (2 * t + 2) * N)
+                nc.sync.dma_start(o_run[:, run], y_run[:, run])
         round_y(nc.vector.tensor_copy, N, N + HALF_N)
         round_y(nc.vector.tensor_copy, N + HALF_N, V - SCALAR_PAIRS)
         round_y(nc.scalar.copy, V - SCALAR_PAIRS, V)
@@ -176,5 +178,4 @@ def tile_picked_siam_abs_po_kernel(tc, x_words, x_scales, w1, w2_words, w2_scale
 
         nc.sync.dma_start(o1, yc[:].bitcast(I32))
         for q in range(QUADRANTS):
-            queue = nc.sync if q % 2 else nc.scalar
-            queue.dma_start(out_2[0, 4 * q : 4 * q + 4, :].bitcast(I32), ys[32 * q : 32 * q + 4, :].bitcast(I32))
+            nc.sync.dma_start(out_2[0, 4 * q : 4 * q + 4, :].bitcast(I32), ys[32 * q : 32 * q + 4, :].bitcast(I32))

@@ -73,7 +73,7 @@ def tile_picked_siam_abs_po_kernel(tc, x_words, x_scales, w1, w2_words, w2_scale
         for q in range(QUADRANTS):
             nc.sync.dma_start(gs[32 * q : 32 * q + 4, :].bitcast(I32), spread[32 * q : 32 * q + 32 : 8, :].bitcast(I32))
 
-        for i, width in enumerate((S, S, N)):
+        for i, width in enumerate((S, S)):
             warm = psum.tile([WARM_M, width], F32, name="warm%d" % i, tag="o%d" % i)
             nc.tensor.matmul_mx(out=warm[:], lhsT=gw[:, :WARM_M].bitcast(FP8X4), lhsT_scale=spread[:, :WARM_M],
                                 rhs=gw[:, :width].bitcast(FP8X4), rhs_scale=spread[:, :width], start=True, stop=True)

from contextlib import ExitStack

import concourse.mybir as mybir

F32 = mybir.dt.float32
BF16 = mybir.dt.bfloat16
I32 = mybir.dt.int32
U32 = mybir.dt.uint32
U16 = mybir.dt.uint16
U8 = mybir.dt.uint8
FP8X4 = mybir.dt.float8_e4m3fn_x4
FP4X4 = mybir.dt.float4_e2m1fn_x4
ALU = mybir.AluOpType
ACT = mybir.ActivationFunctionType

K, T, S, V, H = 512, 1024, 512, 256, 512
P = 128
PACK = 4
QUADRANTS = 4
N = 128
HALF_N = N // 2
HALF_M = P // 2
SCALAR_PLACES = (36, 24)
SCALAR_PAIRS = 32
WARM_M = 32
FLOPS = 2 * K * H * S + 2 * H * H * V


def tile_picked_siam_abs_po_kernel(tc, x_words, x_scales, w1, w2_words, w2_scales, offs, out_0, out_1, out_2):
    nc = tc.nc
    with ExitStack() as ctx:
        keep = ctx.enter_context(tc.tile_pool(name="keep", bufs=1))
        reuse = ctx.enter_context(tc.tile_pool(name="reuse", bufs=1))
        psum = ctx.enter_context(tc.psum_pool(name="psum", bufs=1))

        def sb(shape, dtype, name):
            return keep.tile(shape, dtype, name=name, tag=name, align_bytes=64)

        offsets = sb([P, S // 16], U16, "offsets")
        xw = sb([P, T], U32, "xw")
        xs = sb([P, T], U8, "xs")
        w2s = sb([P, H], U8, "w2s")
        gs = sb([P, S], U8, "gs")
        gw = sb([P, S], U32, "gw")

        nc.vector.memset(xs[:].bitcast(I32), 0)
        nc.vector.memset(w2s[:].bitcast(I32), 0)
        nc.vector.memset(gs[:].bitcast(I32), 0)

        xv = x_words[0].rearrange("p c r -> p (c r)").bitcast(I32)
        nc.sync.dma_start(xw[:, : T // 2].bitcast(I32), xv[:, : T // 2])
        nc.sync.dma_start(offsets[:], offs)
        nc.sync.dma_start(xs[0:P:8, :].bitcast(I32), x_scales[0].bitcast(I32))
        nc.sync.dma_start(xw[:, T // 2 :].bitcast(I32), xv[:, T // 2 :])

        def load_w2_scales(q):
            nc.sync.dma_start(w2s[32 * q : 32 * q + 4, :].bitcast(I32), w2_scales[0, 4 * q : 4 * q + 4, :].bitcast(I32))

        for q in (0, 2):
            load_w2_scales(q)
        w1v = w1.rearrange("(p j) c -> p j c", j=PACK)
        w1raw = [sb([P, PACK, H // 2], F32, "w1raw%d" % h) for h in range(2)]
        for h in range(2):
            nc.sync.dma_start(w1raw[h][:], w1v[:, :, h * H // 2 : (h + 1) * H // 2])
        w2w = sb([P, 2 * H], U8, "w2w")
        nc.sync.dma_start(w2w[:].bitcast(I32), w2_words[0].bitcast(I32))
        for q in (1, 3):
            load_w2_scales(q)

        spread = sb([P, S], U8, "spread")
        nc.vector.tensor_copy(spread[:], xs[:].indirect(offsets[:]))
        nc.vector.tensor_copy(gw[:], xw[:].indirect(offsets[:]))
        for q in range(QUADRANTS):
            nc.sync.dma_start(gs[32 * q : 32 * q + 4, :].bitcast(I32), spread[32 * q : 32 * q + 32 : 8, :].bitcast(I32))

        for i, width in enumerate((S, S)):
            warm = psum.tile([WARM_M, width], F32, name="warm%d" % i, tag="o%d" % i)
            nc.tensor.matmul_mx(out=warm[:], lhsT=gw[:, :WARM_M].bitcast(FP8X4), lhsT_scale=spread[:, :WARM_M],
                                rhs=gw[:, :width].bitcast(FP8X4), rhs_scale=spread[:, :width], start=True, stop=True)

        w1g = reuse.tile([P, PACK, P, PACK], BF16, name="w1g", offset=0, align_bytes=64)
        w1c = sb([P, H], U32, "w1c")
        w1s = sb([P, H], U8, "w1s")

        def round_w1(h, tiles):
            src = w1raw[h][:].rearrange("p j (m t) -> p m j t", t=PACK)[:, :, :, tiles]
            dst = w1g[:].rearrange("p t m j -> p m j t")[:, h * HALF_M : (h + 1) * HALF_M, :, tiles]
            nc.scalar.copy(dst[:, : SCALAR_PLACES[h]], src[:, : SCALAR_PLACES[h]])
            nc.vector.tensor_copy(dst[:, SCALAR_PLACES[h] :], src[:, SCALAR_PLACES[h] :])

        def quantise_w1(h, t):
            cols = slice(t * P + h * HALF_M, t * P + (h + 1) * HALF_M)
            nc.vector.quantize_mx(out=w1c[:, cols].bitcast(FP8X4), scales=w1s[:, cols],
                                  in_=w1g[:, t, h * HALF_M : (h + 1) * HALF_M].rearrange("p m j -> p (m j)"))

        round_w1(0, slice(0, PACK))
        for t in range(PACK):
            quantise_w1(0, t)
        for u in range(2):
            round_w1(1, slice(2 * u, 2 * u + 2))
        for t in range(PACK):
            quantise_w1(1, t)

        w2d = reuse.tile([P, PACK, P], U8, name="w2d", offset=0, align_bytes=64)
        nc.vector.tensor_copy(w2d[:].rearrange("p t m -> p m t"), w2s[:].rearrange("p (m t) -> p m t", t=PACK))
        w2c = sb([P, PACK, 2 * P], U8, "w2c")
        nc.scalar.copy(w2c[:].bitcast(U16).rearrange("p t m -> p m t"), w2w[:].bitcast(U16).rearrange("p (m t) -> p m t", t=PACK))

        chunks = range(V // N)
        first = {(side, c): psum.tile([P, PACK, N], F32, name="h%d%d" % (side, c), tag="h%d%d" % (side, c)) for side in range(2) for c in chunks}
        for c in chunks:
            for side in range(2):
                picked = slice(side * V + c * N, side * V + (c + 1) * N)
                for t in range(PACK):
                    cols = slice(t * P, (t + 1) * P)
                    nc.tensor.matmul_mx(out=first[side, c][:, t, :], lhsT=w1c[:, cols].bitcast(FP8X4), lhsT_scale=w1s[:, cols],
                                        rhs=gw[:, picked].bitcast(FP8X4), rhs_scale=gs[:, picked], start=True, stop=True)

        zc, zs = {}, {}
        for c in chunks:
            a, b = first[0, c], first[1, c]
            z = sb([P, N * PACK], BF16, "z%d" % c)
            for e in range(2):
                ns = slice(e * HALF_N, (e + 1) * HALF_N)
                ra = sb([P, HALF_N, PACK], F32, "ra%d%d" % (c, e))
                nc.scalar.activation(ra[:], a[:].rearrange("p t n -> p n t")[:, ns], ACT.Relu)
                d = sb([P, HALF_N, PACK], F32, "d%d%d" % (c, e))
                nc.vector.scalar_tensor_tensor(d[:], b[:].rearrange("p t n -> p n t")[:, ns], 0.0, ra[:], ALU.max, ALU.subtract)
                nc.scalar.activation(z[:, ns.start * PACK : ns.stop * PACK], d[:].rearrange("p n t -> p (n t)"), ACT.Abs)
            zc[c] = sb([P, N], U32, "zc%d" % c)
            zs[c] = sb([P, N], U8, "zs%d" % c)
            step = HALF_N if c == chunks[-1] else N
            for n0 in range(0, N, step):
                nc.vector.quantize_mx(out=zc[c][:, n0 : n0 + step].bitcast(FP8X4), scales=zs[c][:, n0 : n0 + step],
                                      in_=z[:, n0 * PACK : (n0 + step) * PACK])

        yc = sb([P, V], U32, "yc")
        ys = sb([P, V], U8, "ys")
        o0 = out_0.rearrange("(p t) v -> p t v", t=PACK)
        o1 = out_1[0].rearrange("p c r -> p (c r)").bitcast(I32)
        yb = sb([P, V, PACK], BF16, "yb")
        y = sb([P, PACK, V], F32, "y")

        def quantise_y(n0, n1):
            nc.vector.quantize_mx(out=yc[:, n0:n1].bitcast(FP8X4), scales=ys[:, n0:n1], in_=yb[:, n0:n1].rearrange("p n t -> p (n t)"))

        def product(bank, t, c):
            nc.tensor.matmul_mx(out=bank, lhsT=w2c[:, t, :].bitcast(FP4X4), lhsT_scale=w2d[:, t, :],
                                rhs=zc[c][:].bitcast(FP8X4), rhs_scale=zs[c][:], start=True, stop=True)

        def round_y(copy, n0, n1):
            copy(yb[:, n0:n1].rearrange("p (n i) t -> p n t i", i=4), y[:, :, n0:n1].rearrange("p t (n i) -> p n t i", i=4))

        y_run = y[:].rearrange("p t v -> p (t v)")
        o_run = o0.rearrange("p t v -> p (t v)")
        for u in range(2):
            bank = psum.tile([P, 2, N], F32, name="o0%d" % u, tag="o%d" % u)
            for e in range(2):
                product(bank[:, e, :], u + 2 * e, 0)
            empty = nc.scalar.copy if u else nc.vector.tensor_copy
            empty(y[:, u::2, :N], bank[:])
        nc.sync.dma_start(o0[:, ::2, :N], y[:, ::2, :N])
        round_y(nc.vector.tensor_copy, 0, N)
        for t, tag in enumerate(("o2", "o3", "h00", "h10")):
            bank = psum.tile([P, N], F32, name="o1%d" % t, tag=tag)
            product(bank[:], t, 1)
            empty = nc.scalar.copy if t % 2 else nc.vector.tensor_copy
            empty(y[:, t, N:], bank[:])
            if t % 2:
                run = slice((2 * t - 1) * N, (2 * t + 2) * N)
                nc.sync.dma_start(o_run[:, run], y_run[:, run])
        round_y(nc.vector.tensor_copy, N, N + HALF_N)
        round_y(nc.vector.tensor_copy, N + HALF_N, V - SCALAR_PAIRS)
        round_y(nc.scalar.copy, V - SCALAR_PAIRS, V)
        quantise_y(0, N)
        quantise_y(N, N + HALF_N)
        quantise_y(N + HALF_N, V)

        nc.sync.dma_start(o1, yc[:].bitcast(I32))
        for q in range(QUADRANTS):
            nc.sync.dma_start(out_2[0, 4 * q : 4 * q + 4, :].bitcast(I32), ys[32 * q : 32 * q + 4, :].bitcast(I32))
